import numpy as np
import ml_dtypes


def mxq(x, axis, fmt="e4m3"):
    dtype, down = {"e4m3": (ml_dtypes.float8_e4m3fn, 7), "e5m2": (ml_dtypes.float8_e5m2, 14)}[fmt]
    v = np.moveaxis(np.asarray(x, np.float32).astype(ml_dtypes.bfloat16).astype(np.float64), axis, -1)
    blocks = v.reshape(v.shape[:-1] + (-1, 32))
    amax = np.abs(blocks).max(-1, keepdims=True)
    byte = np.maximum(np.where(amax > 0, np.frexp(amax)[1] - 1 + 127, 0) - down, 1)
    scale = np.exp2(byte - 127.0)
    codes = (blocks / scale).astype(np.float32).astype(dtype).astype(np.float64)
    return np.moveaxis((codes * scale).reshape(v.shape), -1, axis)


WIDE = False


def mx_kscale(k):
    if not WIDE:
        return np.ones(k)
    levels = np.array([18, -18])
    if k % 512:
        return np.exp2(np.random.permutation(np.resize(levels, k // 32))).repeat(32)
    a = np.empty((k // 512, 16))
    for p in range(k // 512):
        a[p, :8] = np.random.permutation(np.resize(levels, 8))
        for g in range(8):
            far = levels[np.abs(levels - a[p, g]) >= 10]
            a[p, g + 8] = far[np.random.randint(len(far))]
    return np.exp2(a.ravel()).repeat(32)


def f64(x):
    return np.asarray(x).astype(np.float64)


def striped(idx):
    return np.tile(np.asarray(idx).reshape(-1, 16).T, (8, 1)).astype(np.uint16)


def unstriped(offs):
    return offs[:16].T.reshape(-1).astype(np.int64)


E2M1 = np.array([0.0, 0.5, 1.0, 1.5, 2.0, 3.0, 4.0, 6.0, -0.0, -0.5, -1.0, -1.5, -2.0, -3.0, -4.0, -6.0])


def pack_weight(w, fmt):
    k, n = w.shape
    w = f64(np.asarray(w, np.float32).astype(ml_dtypes.bfloat16)).reshape(k // 32, 32, n)
    amax = np.abs(w).max(1)
    if fmt == "e4m3":
        byte = np.frexp(amax)[1] - 1 + 127 - 7
    else:
        mant, ex = np.frexp(amax / 6.0)
        byte = np.where(mant > 0.5, ex, ex - 1) + 127
    byte = np.clip(np.where(amax > 0, byte, 1), 1, 254)
    scaled = (w * np.exp2(127.0 - byte)[:, None, :]).reshape(k, n).astype(np.float32)
    by_word = np.ascontiguousarray(scaled.reshape(k // 512, 128, 4, n).transpose(0, 1, 3, 2))
    if fmt == "e4m3":
        words = by_word.astype(ml_dtypes.float8_e4m3fn).view(np.uint8)
    else:
        c = by_word.astype(ml_dtypes.float4_e2m1fn).view(np.uint8) & 0xF
        words = (c[..., 0::2] | (c[..., 1::2] << 4)).reshape(k // 512, 128, 2 * n)
    return np.ascontiguousarray(words), np.ascontiguousarray(byte.astype(np.uint8).reshape(k // 512, 16, n))


def unpack_weight(words, scales, fmt):
    g, _, n = scales.shape
    words = np.ascontiguousarray(words).reshape(g, 128, n, -1)
    if fmt == "e4m3":
        vals = words.view(ml_dtypes.float8_e4m3fn).astype(np.float64)
    else:
        nib = np.empty((g, 128, n, 4), np.uint8)
        nib[..., 0::2] = words & 0xF
        nib[..., 1::2] = words >> 4
        vals = E2M1[nib]
    vals = vals * np.repeat(np.exp2(scales.astype(np.float64) - 127.0), 8, axis=1)[..., None]
    return vals.transpose(0, 1, 3, 2).reshape(g * 512, n)


B, N, T, D, DV, NQ = 2, 512, 2048, 256, 512, 512


def setup_inputs():
    n = np.random.standard_normal
    seg = T // B
    idx = np.concatenate([b * seg + np.random.permutation(seg)[:N] for b in range(B)])
    s = mx_kscale(DV)[:, None]
    z = mx_kscale(NQ)[:, None]
    p = np.exp(n((B, NQ, N)))
    p = p / p.mean(2, keepdims=True)
    kp = pack_weight(n((DV, T)) / s, "e4m3")
    return {
        "doT": (n((B, DV, NQ)) * s / np.sqrt(DV)).astype(np.float32),
        "v_words": kp[0],
        "v_scales": kp[1],
        "p": (p * z / np.sqrt(NQ)).astype(np.float32),
        "delta": (0.3 * n((B, NQ, 1))).astype(np.float32),
        "qm": (n((B, NQ, D)) / z).astype(np.float32),
        "offs": striped(idx),
    }


def reference(doT, v_words, v_scales, p, delta, qm, offs):
    idx = unstriped(offs)
    pool = unpack_weight(v_words, v_scales, "e4m3")
    pick = lambda x: x[:, idx].reshape(x.shape[0], B, N).transpose(1, 0, 2)
    dp = mxq(f64(doT), 1, "e5m2").transpose(0, 2, 1) @ pick(pool)
    ds = f64(p) * (dp - f64(delta))
    dk = mxq(f64(qm), 1, "e4m3").transpose(0, 2, 1) @ mxq(ds, 1, "e5m2")
    out = np.zeros((D, T))
    out[:, idx] = dk.transpose(1, 0, 2).reshape(D, B * N)
    return out

@@ -1,0 +1,239 @@
+from contextlib import ExitStack
+
+import concourse.mybir as mybir
+
+B, N, T, D, DV, NQ = 2, 512, 2048, 256, 512, 512
+FLOPS = 2 * B * NQ * N * (DV + D)
+
+F32 = mybir.dt.float32
+BF16 = mybir.dt.bfloat16
+I32 = mybir.dt.int32
+U32 = mybir.dt.uint32
+U16 = mybir.dt.uint16
+U8 = mybir.dt.uint8
+E4 = mybir.dt.float8_e4m3fn_x4
+E5 = mybir.dt.float8_e5m2_x4
+SUB = mybir.AluOpType.subtract
+MULT = mybir.AluOpType.mult
+
+P = 128
+PACK = 4
+SEG = T // B
+HALVES = 2
+RUN = 4
+LIST_ROWS = 16
+
+
+def tile_attend_bwd_seg_kernel(tc, doT, v_words, v_scales, p, delta, qm, offs, out):
+    nc = tc.nc
+    with ExitStack() as ctx:
+        sb = ctx.enter_context(tc.tile_pool(name="sb", bufs=1))
+        ps = ctx.enter_context(tc.psum_pool(name="ps", bufs=1))
+
+        def new(name, shape, dtype, tag=None):
+            return sb.tile(shape, dtype, name=name, tag=tag or name, align_bytes=64)
+
+        offsets = sb.tile([P, B * N // LIST_ROWS], U16, name="offsets")
+        pool_words = new("pool_words", [P, T], U32)
+        pool_scales = new("pool_scales", [P, T], U8)
+        delta_sb = new("delta_sb", [P, B, PACK], F32)
+        do_raw = [[new(f"do_raw{b}{h}", [P, PACK, NQ // HALVES], F32) for h in range(HALVES)] for b in range(B)]
+        p_sb = [[new(f"p_sb{b}{h}", [P, PACK, N // HALVES], F32) for h in range(HALVES)] for b in range(B)]
+        q_raw = [new(f"q_raw{b}", [P, PACK, D], F32) for b in range(B)]
+        window = [[new(f"window{b}{h}", [P, (b + 1) * SEG], F32) for h in range(D // P)] for b in range(B)]
+        v_codes = [new(f"v_codes{b}", [P, N], U32) for b in range(B)]
+        v_plane = [new(f"v_plane{b}", [P, N], U8) for b in range(B)]
+        do_bf = [new(f"do_bf{b}", [P, PACK, P, PACK], BF16) for b in range(B)]
+        do_codes = [new(f"do_codes{b}", [P, NQ], U32) for b in range(B)]
+        do_plane = [new(f"do_plane{b}", [P, NQ], U8) for b in range(B)]
+        q_bf = [new(f"q_bf{b}", [P, D, PACK], BF16) for b in range(B)]
+        q_codes = [new(f"q_codes{b}", [P, D], U32) for b in range(B)]
+        q_plane = [new(f"q_plane{b}", [P, D], U8) for b in range(B)]
+        ds_rows = [[new(f"ds_rows{b}{h}", [P, PACK, N // HALVES], BF16) for h in range(HALVES)] for b in range(B)]
+        ds_bf = [[new(f"ds_bf{b}{h}", [P, N // HALVES, PACK], BF16) for h in range(HALVES)] for b in range(B)]
+        ds_codes = [new(f"ds_codes{b}", [P, N], U32) for b in range(B)]
+        ds_plane = [new(f"ds_plane{b}", [P, N], U8) for b in range(B)]
+        dp_ps = [ps.tile([P, N], F32, name=f"dp_ps{r}") for r in range(PACK)]
+        dk_ps = [[ps.tile([P, N], F32, name=f"dk_ps{b}{h}") for h in range(D // P)] for b in range(B)]
+
+        words_hbm = v_words[0].rearrange("g t r -> g (t r)").bitcast(I32)
+        scales_hbm = v_scales[0].bitcast(I32)
+
+        def slots(b, lo=0, hi=N):
+            return offsets[:, (b * N + lo) // LIST_ROWS : (b * N + hi) // LIST_ROWS]
+
+        def half(h, width):
+            return slice(h * width // HALVES, (h + 1) * width // HALVES)
+
+        def load_words(b):
+            cols = slice(b * SEG, (b + 1) * SEG)
+            nc.sync.dma_start(out=pool_words[:, cols].bitcast(I32), in_=words_hbm[:, cols])
+
+        def load_do(b, h):
+            rows = doT[b].rearrange("(g j) q -> g j q", j=PACK)
+            nc.sync.dma_start(out=do_raw[b][h][:], in_=rows[:, :, half(h, NQ)])
+
+        def load_p(b, h):
+            rows = p[b].rearrange("(s r) i -> s r i", r=PACK)
+            nc.sync.dma_start(out=p_sb[b][h][:], in_=rows[:, :, half(h, N)])
+
+        def load_q(b):
+            nc.sync.dma_start(out=q_raw[b][:], in_=qm[b].rearrange("(s r) d -> s r d", r=PACK))
+
+        def cast_do(b, h):
+            nc.scalar.copy(
+                out=do_bf[b][:, :, half(h, P), :].rearrange("g r s j -> g s j r"),
+                in_=do_raw[b][h][:].rearrange("g j (s r) -> g s j r", r=PACK),
+            )
+
+        def interleave(dst, src):
+            nc.scalar.copy(
+                out=dst[:].rearrange("s (c i) r -> s c r i", i=RUN),
+                in_=src[:].rearrange("s r (c i) -> s c r i", i=RUN),
+            )
+
+        def gather_words(b):
+            nc.vector.tensor_copy(v_codes[b][:], pool_words[:, 0 : (b + 1) * SEG].indirect(slots(b)))
+
+        def gather_scales(b):
+            nc.vector.tensor_copy(v_plane[b][:], pool_scales[:, 0 : (b + 1) * SEG].indirect(slots(b)))
+
+        def quantize_do(b):
+            nc.vector.quantize_mx(
+                out=do_codes[b][:].bitcast(E5),
+                scales=do_plane[b][:],
+                in_=do_bf[b][:].rearrange("g r s j -> g (r s j)"),
+            )
+
+        def quantize_q(b):
+            nc.vector.quantize_mx(
+                out=q_codes[b][:].bitcast(E4),
+                scales=q_plane[b][:],
+                in_=q_bf[b][:].rearrange("s d r -> s (d r)"),
+            )
+
+        def quantize_ds(b, h):
+            nc.vector.quantize_mx(
+                out=ds_codes[b][:, half(h, N)].bitcast(E5),
+                scales=ds_plane[b][:, half(h, N)],
+                in_=ds_bf[b][h][:].rearrange("s i r -> s (i r)"),
+            )
+
+        def product_dp(b):
+            for r in range(PACK):
+                cols = slice(r * P, (r + 1) * P)
+                nc.tensor.matmul_mx(
+                    out=dp_ps[r][:],
+                    lhsT=do_codes[b][:, cols].bitcast(E5),
+                    lhsT_scale=do_plane[b][:, cols],
+                    rhs=v_codes[b][:].bitcast(E4),
+                    rhs_scale=v_plane[b][:],
+                    start=True,
+                    stop=True,
+                )
+
+        def form_ds(b, h):
+            for r in range(PACK):
+                nc.vector.scalar_tensor_tensor(
+                    out=ds_rows[b][h][:, r, :],
+                    in0=dp_ps[r][:, half(h, N)],
+                    scalar=delta_sb[:, b, r : r + 1],
+                    in1=p_sb[b][h][:, r, :],
+                    op0=SUB,
+                    op1=MULT,
+                )
+
+        def interleave_ds(b, h):
+            interleave(ds_bf[b][h], ds_rows[b][h])
+
+        def product_dk(b):
+            for h in range(D // P):
+                cols = slice(h * P, (h + 1) * P)
+                nc.tensor.matmul_mx(
+                    out=dk_ps[b][h][:],
+                    lhsT=q_codes[b][:, cols].bitcast(E4),
+                    lhsT_scale=q_plane[b][:, cols],
+                    rhs=ds_codes[b][:].bitcast(E5),
+                    rhs_scale=ds_plane[b][:],
+                    start=True,
+                    stop=True,
+                )
+
+        def copy_out(b, h, part, tag=None):
+            staged = new(f"dk_sb{b}{h}{part}", [P, N // HALVES], F32, tag)
+            nc.scalar.copy(out=staged[:], in_=dk_ps[b][h][:, half(part, N)])
+            return staged
+
+        def scatter(b, h, part, staged):
+            cols = half(part, N)
+            nc.vector.tensor_copy(window[b][h][:].indirect(slots(b, cols.start, cols.stop)), staged[:])
+
+        def store(b, h):
+            cols = slice(b * SEG, (b + 1) * SEG)
+            nc.sync.dma_start(out=out[h * P : (h + 1) * P, cols], in_=window[b][h][:, cols])
+
+        nc.vector.memset(pool_scales[:].bitcast(I32), 0)
+        nc.sync.dma_start(offsets[:], offs)
+        for quad in range(4):
+            nc.sync.dma_start(
+                out=pool_scales[32 * quad : 32 * quad + 4, :].bitcast(I32),
+                in_=scales_hbm[4 * quad : 4 * quad + 4, :],
+            )
+        load_do(0, 0)
+        load_do(0, 1)
+        load_words(0)
+        load_p(0, 0)
+        nc.sync.dma_start(out=delta_sb[:], in_=delta.rearrange("b (s r) o -> s b (r o)", r=PACK))
+        load_q(0)
+        load_p(0, 1)
+        load_words(1)
+        load_do(1, 0)
+        load_do(1, 1)
+        load_p(1, 0)
+        load_p(1, 1)
+        load_q(1)
+        for b in range(B):
+            for h in range(D // P):
+                nc.vector.memset(window[b][h][:, b * SEG : (b + 1) * SEG].bitcast(I32), 0)
+
+        cast_do(0, 0)
+        cast_do(0, 1)
+        gather_scales(0)
+        quantize_do(0)
+        gather_words(0)
+        product_dp(0)
+        interleave(q_bf[0], q_raw[0])
+        form_ds(0, 0)
+        interleave_ds(0, 0)
+        form_ds(0, 1)
+        interleave_ds(0, 1)
+        quantize_q(0)
+        quantize_ds(0, 0)
+        quantize_ds(0, 1)
+        product_dk(0)
+        gather_scales(1)
+        gather_words(1)
+        scatter(0, 0, 0, copy_out(0, 0, 0))
+        cast_do(1, 0)
+        cast_do(1, 1)
+        quantize_do(1)
+        product_dp(1)
+        scatter(0, 0, 1, copy_out(0, 0, 1, "do_raw11"))
+        store(0, 0)
+        interleave(q_bf[1], q_raw[1])
+        form_ds(1, 0)
+        staged = copy_out(0, 1, 0, "p_sb10")
+        interleave_ds(1, 0)
+        form_ds(1, 1)
+        interleave_ds(1, 1)
+        quantize_q(1)
+        scatter(0, 1, 0, staged)
+        quantize_ds(1, 0)
+        quantize_ds(1, 1)
+        product_dk(1)
+        scatter(0, 1, 1, copy_out(0, 1, 1, "ds_rows11"))
+        store(0, 1)
+        for h in range(D // P):
+            for part in range(HALVES):
+                scatter(1, h, part, copy_out(1, h, part))
+            store(1, h)

@@ -36,12 +36,13 @@ def tile_attend_bwd_seg_kernel(tc, doT, v_words, v_scales, p, delta, qm, offs, o
         offsets = sb.tile([P, B * N // LIST_ROWS], U16, name="offsets")
         pool_words = new("pool_words", [P, T], U32)
         pool_scales = new("pool_scales", [P, T], U8)
+        landed_scales = new("landed_scales", [P, T], U8)
         delta_sb = new("delta_sb", [P, B, PACK], F32)
         do_raw = [[new(f"do_raw{b}{h}", [P, PACK, NQ // HALVES], F32) for h in range(HALVES)] for b in range(B)]
         p_sb = [[new(f"p_sb{b}{h}", [P, PACK, N // HALVES], F32) for h in range(HALVES)] for b in range(B)]
         q_raw = [new(f"q_raw{b}", [P, PACK, D], F32) for b in range(B)]
-        window = [[new(f"window{b}{h}", [P, (b + 1) * SEG], F32) for h in range(D // P)] for b in range(B)]
-        v_codes = [new(f"v_codes{b}", [P, N], U32) for b in range(B)]
+        window = [{}, {}]
+        v_codes = {}
         v_plane = [new(f"v_plane{b}", [P, N], U8) for b in range(B)]
         do_bf = [new(f"do_bf{b}", [P, PACK, P, PACK], BF16) for b in range(B)]
         do_codes = [new(f"do_codes{b}", [P, NQ], U32) for b in range(B)]
@@ -65,6 +66,10 @@ def tile_attend_bwd_seg_kernel(tc, doT, v_words, v_scales, p, delta, qm, offs, o
         def half(h, width):
             return slice(h * width // HALVES, (h + 1) * width // HALVES)
 
+        def clear_window(b, h, tag=None):
+            window[b][h] = new(f"window{b}{h}", [P, (b + 1) * SEG], F32, tag)
+            nc.vector.memset(window[b][h][:, b * SEG : (b + 1) * SEG].bitcast(I32), 0)
+
         def load_words(b):
             cols = slice(b * SEG, (b + 1) * SEG)
             nc.sync.dma_start(out=pool_words[:, cols].bitcast(I32), in_=words_hbm[:, cols])
@@ -86,24 +91,26 @@ def tile_attend_bwd_seg_kernel(tc, doT, v_words, v_scales, p, delta, qm, offs, o
                 in_=do_raw[b][h][:].rearrange("g j (s r) -> g s j r", r=PACK),
             )
 
-        def interleave(dst, src):
-            nc.scalar.copy(
+        def interleave(dst, src, copy=nc.scalar.copy):
+            copy(
                 out=dst[:].rearrange("s (c i) r -> s c r i", i=RUN),
                 in_=src[:].rearrange("s r (c i) -> s c r i", i=RUN),
             )
 
-        def gather_words(b):
+        def gather_words(b, tag=None):
+            v_codes[b] = new(f"v_codes{b}", [P, N], U32, tag)
             nc.vector.tensor_copy(v_codes[b][:], pool_words[:, 0 : (b + 1) * SEG].indirect(slots(b)))
 
         def gather_scales(b):
             nc.vector.tensor_copy(v_plane[b][:], pool_scales[:, 0 : (b + 1) * SEG].indirect(slots(b)))
 
         def quantize_do(b):
-            nc.vector.quantize_mx(
-                out=do_codes[b][:].bitcast(E5),
-                scales=do_plane[b][:],
-                in_=do_bf[b][:].rearrange("g r s j -> g (r s j)"),
-            )
+            for h in range(HALVES):
+                nc.vector.quantize_mx(
+                    out=do_codes[b][:, half(h, NQ)].bitcast(E5),
+                    scales=do_plane[b][:, half(h, NQ)],
+                    in_=do_bf[b][:, half(h, PACK), :, :].rearrange("g r s j -> g (r s j)"),
+                )
 
         def quantize_q(b):
             nc.vector.quantize_mx(
@@ -132,8 +139,8 @@ def tile_attend_bwd_seg_kernel(tc, doT, v_words, v_scales, p, delta, qm, offs, o
                     stop=True,
                 )
 
-        def form_ds(b, h):
-            for r in range(PACK):
+        def form_ds(b, steps):
+            for r, h in steps:
                 nc.vector.scalar_tensor_tensor(
                     out=ds_rows[b][h][:, r, :],
                     in0=dp_ps[r][:, half(h, N)],
@@ -143,8 +150,8 @@ def tile_attend_bwd_seg_kernel(tc, doT, v_words, v_scales, p, delta, qm, offs, o
                     op1=MULT,
                 )
 
-        def interleave_ds(b, h):
-            interleave(ds_bf[b][h], ds_rows[b][h])
+        def interleave_ds(b, h, copy=nc.scalar.copy):
+            interleave(ds_bf[b][h], ds_rows[b][h], copy)
 
         def product_dk(b):
             for h in range(D // P):
@@ -159,14 +166,13 @@ def tile_attend_bwd_seg_kernel(tc, doT, v_words, v_scales, p, delta, qm, offs, o
                     stop=True,
                 )
 
-        def copy_out(b, h, part, tag=None):
-            staged = new(f"dk_sb{b}{h}{part}", [P, N // HALVES], F32, tag)
-            nc.scalar.copy(out=staged[:], in_=dk_ps[b][h][:, half(part, N)])
-            return staged
+        def copy_out(b, h, lo, hi, tag=None):
+            staged = new(f"dk_sb{b}{h}_{lo}", [P, hi - lo], F32, tag)
+            nc.scalar.copy(out=staged[:], in_=dk_ps[b][h][:, lo:hi])
+            return b, h, lo, hi, staged
 
-        def scatter(b, h, part, staged):
-            cols = half(part, N)
-            nc.vector.tensor_copy(window[b][h][:].indirect(slots(b, cols.start, cols.stop)), staged[:])
+        def scatter(b, h, lo, hi, staged):
+            nc.vector.tensor_copy(window[b][h][:].indirect(slots(b, lo, hi)), staged[:])
 
         def store(b, h):
             cols = slice(b * SEG, (b + 1) * SEG)
@@ -175,65 +181,68 @@ def tile_attend_bwd_seg_kernel(tc, doT, v_words, v_scales, p, delta, qm, offs, o
         nc.vector.memset(pool_scales[:].bitcast(I32), 0)
         nc.sync.dma_start(offsets[:], offs)
         for quad in range(4):
-            nc.sync.dma_start(
-                out=pool_scales[32 * quad : 32 * quad + 4, :].bitcast(I32),
+            nc.scalar.dma_start(
+                out=landed_scales[32 * quad : 32 * quad + 4, :].bitcast(I32),
                 in_=scales_hbm[4 * quad : 4 * quad + 4, :],
             )
+        load_words(0)
         load_do(0, 0)
         load_do(0, 1)
-        load_words(0)
         load_p(0, 0)
         nc.sync.dma_start(out=delta_sb[:], in_=delta.rearrange("b (s r) o -> s b (r o)", r=PACK))
-        load_q(0)
         load_p(0, 1)
+        load_q(0)
         load_words(1)
         load_do(1, 0)
         load_do(1, 1)
         load_p(1, 0)
         load_p(1, 1)
         load_q(1)
-        for b in range(B):
-            for h in range(D // P):
-                nc.vector.memset(window[b][h][:, b * SEG : (b + 1) * SEG].bitcast(I32), 0)
+        clear_window(0, 0)
+        clear_window(0, 1)
+        clear_window(1, 0)
+        for quad in range(4):
+            rows = slice(32 * quad, 32 * quad + 4)
+            nc.vector.tensor_copy(pool_scales[rows, :].bitcast(I32), landed_scales[rows, :].bitcast(I32))
 
+        steps = [(r, h) for r in range(PACK) for h in range(HALVES)]
+        gather_words(0)
+        gather_scales(0)
         cast_do(0, 0)
         cast_do(0, 1)
-        gather_scales(0)
         quantize_do(0)
-        gather_words(0)
         product_dp(0)
+        gather_scales(1)
+        clear_window(1, 1, "do_raw01")
         interleave(q_bf[0], q_raw[0])
-        form_ds(0, 0)
+        form_ds(0, steps)
         interleave_ds(0, 0)
-        form_ds(0, 1)
-        interleave_ds(0, 1)
         quantize_q(0)
+        interleave_ds(0, 1, nc.vector.tensor_copy)
         quantize_ds(0, 0)
         quantize_ds(0, 1)
         product_dk(0)
-        gather_scales(1)
-        gather_words(1)
-        scatter(0, 0, 0, copy_out(0, 0, 0))
+        gather_words(1, "ds_bf00")
+        piece = copy_out(0, 0, 0, 320)
+        scatter(*piece)
         cast_do(1, 0)
         cast_do(1, 1)
         quantize_do(1)
         product_dp(1)
-        scatter(0, 0, 1, copy_out(0, 0, 1, "do_raw11"))
+        scatter(*copy_out(0, 0, 320, N, "do_raw11"))
         store(0, 0)
         interleave(q_bf[1], q_raw[1])
-        form_ds(1, 0)
-        staged = copy_out(0, 1, 0, "p_sb10")
+        form_ds(1, steps)
+        piece = copy_out(0, 1, 0, 224, "p_sb10")
         interleave_ds(1, 0)
-        form_ds(1, 1)
         interleave_ds(1, 1)
         quantize_q(1)
-        scatter(0, 1, 0, staged)
+        scatter(*piece)
         quantize_ds(1, 0)
         quantize_ds(1, 1)
         product_dk(1)
-        scatter(0, 1, 1, copy_out(0, 1, 1, "ds_rows11"))
+        scatter(*copy_out(0, 1, 224, N, "ds_rows11"))
         store(0, 1)
         for h in range(D // P):
-            for part in range(HALVES):
-                scatter(1, h, part, copy_out(1, h, part))
+            scatter(*copy_out(1, h, 0, N))
             store(1, h)

@@ -20,7 +20,6 @@ P = 128
 PACK = 4
 SEG = T // B
 HALVES = 2
-RUN = 4
 LIST_ROWS = 16
 
 
@@ -38,8 +37,8 @@ def tile_attend_bwd_seg_kernel(tc, doT, v_words, v_scales, p, delta, qm, offs, o
         pool_scales = new("pool_scales", [P, T], U8)
         landed_scales = new("landed_scales", [P, T], U8)
         delta_sb = new("delta_sb", [P, B, PACK], F32)
-        do_raw = [[new(f"do_raw{b}{h}", [P, PACK, NQ // HALVES], F32) for h in range(HALVES)] for b in range(B)]
-        p_sb = [[new(f"p_sb{b}{h}", [P, PACK, N // HALVES], F32) for h in range(HALVES)] for b in range(B)]
+        do_raw = [new(f"do_raw{b}", [P, PACK, NQ], F32) for b in range(B)]
+        p_sb = [[new(f"p_sb{b}{h}", [P, PACK // HALVES, N], F32) for h in range(HALVES)] for b in range(B)]
         q_raw = [new(f"q_raw{b}", [P, PACK, D], F32) for b in range(B)]
         window = [{}, {}]
         v_codes = {}
@@ -50,7 +49,7 @@ def tile_attend_bwd_seg_kernel(tc, doT, v_words, v_scales, p, delta, qm, offs, o
         q_bf = [new(f"q_bf{b}", [P, D, PACK], BF16) for b in range(B)]
         q_codes = [new(f"q_codes{b}", [P, D], U32) for b in range(B)]
         q_plane = [new(f"q_plane{b}", [P, D], U8) for b in range(B)]
-        ds_rows = [[new(f"ds_rows{b}{h}", [P, PACK, N // HALVES], BF16) for h in range(HALVES)] for b in range(B)]
+        ds_rows = [new(f"ds_rows{b}", [P, PACK, N], BF16) for b in range(B)]
         ds_bf = [[new(f"ds_bf{b}{h}", [P, N // HALVES, PACK], BF16) for h in range(HALVES)] for b in range(B)]
         ds_codes = [new(f"ds_codes{b}", [P, N], U32) for b in range(B)]
         ds_plane = [new(f"ds_plane{b}", [P, N], U8) for b in range(B)]
@@ -66,36 +65,33 @@ def tile_attend_bwd_seg_kernel(tc, doT, v_words, v_scales, p, delta, qm, offs, o
         def half(h, width):
             return slice(h * width // HALVES, (h + 1) * width // HALVES)
 
-        def clear_window(b, h, tag=None):
+        def clear_window(b, h, engine=nc.vector, tag=None):
             window[b][h] = new(f"window{b}{h}", [P, (b + 1) * SEG], F32, tag)
-            nc.vector.memset(window[b][h][:, b * SEG : (b + 1) * SEG].bitcast(I32), 0)
+            engine.memset(window[b][h][:, b * SEG : (b + 1) * SEG].bitcast(I32), 0)
 
         def load_words(b):
             cols = slice(b * SEG, (b + 1) * SEG)
             nc.sync.dma_start(out=pool_words[:, cols].bitcast(I32), in_=words_hbm[:, cols])
 
-        def load_do(b, h):
-            rows = doT[b].rearrange("(g j) q -> g j q", j=PACK)
-            nc.sync.dma_start(out=do_raw[b][h][:], in_=rows[:, :, half(h, NQ)])
-
-        def load_p(b, h):
-            rows = p[b].rearrange("(s r) i -> s r i", r=PACK)
-            nc.sync.dma_start(out=p_sb[b][h][:], in_=rows[:, :, half(h, N)])
+        def load_do(b):
+            nc.sync.dma_start(out=do_raw[b][:], in_=doT[b].rearrange("(g j) q -> g j q", j=PACK))
 
         def load_q(b):
             nc.sync.dma_start(out=q_raw[b][:], in_=qm[b].rearrange("(s r) d -> s r d", r=PACK))
 
+        def load_p(b):
+            rows = p[b].rearrange("(s r) i -> s r i", r=PACK)
+            for h in range(HALVES):
+                nc.sync.dma_start(out=p_sb[b][h][:], in_=rows[:, half(h, PACK), :])
+
         def cast_do(b, h):
             nc.scalar.copy(
-                out=do_bf[b][:, :, half(h, P), :].rearrange("g r s j -> g s j r"),
-                in_=do_raw[b][h][:].rearrange("g j (s r) -> g s j r", r=PACK),
+                out=do_bf[b][:, half(h, PACK), :, :].rearrange("g r s j -> g s j r"),
+                in_=do_raw[b][:].rearrange("g j (s r) -> g s j r", r=PACK)[:, :, :, half(h, PACK)],
             )
 
         def interleave(dst, src, copy=nc.scalar.copy):
-            copy(
-                out=dst[:].rearrange("s (c i) r -> s c r i", i=RUN),
-                in_=src[:].rearrange("s r (c i) -> s c r i", i=RUN),
-            )
+            copy(out=dst, in_=src.rearrange("s r x -> s x r"))
 
         def gather_words(b, tag=None):
             v_codes[b] = new(f"v_codes{b}", [P, N], U32, tag)
@@ -139,19 +135,20 @@ def tile_attend_bwd_seg_kernel(tc, doT, v_words, v_scales, p, delta, qm, offs, o
                     stop=True,
                 )
 
-        def form_ds(b, steps):
-            for r, h in steps:
+        def form_ds(b):
+            steps = [(r, slice(0, N)) for r in range(PACK - 1)] + [(PACK - 1, half(h, N)) for h in range(HALVES)]
+            for r, cols in steps:
                 nc.vector.scalar_tensor_tensor(
-                    out=ds_rows[b][h][:, r, :],
-                    in0=dp_ps[r][:, half(h, N)],
+                    out=ds_rows[b][:, r, cols],
+                    in0=dp_ps[r][:, cols],
                     scalar=delta_sb[:, b, r : r + 1],
-                    in1=p_sb[b][h][:, r, :],
+                    in1=p_sb[b][r // HALVES][:, r % HALVES, cols],
                     op0=SUB,
                     op1=MULT,
                 )
 
         def interleave_ds(b, h, copy=nc.scalar.copy):
-            interleave(ds_bf[b][h], ds_rows[b][h], copy)
+            interleave(ds_bf[b][h][:], ds_rows[b][:, :, half(h, N)], copy)
 
         def product_dk(b):
             for h in range(D // P):
@@ -178,44 +175,38 @@ def tile_attend_bwd_seg_kernel(tc, doT, v_words, v_scales, p, delta, qm, offs, o
             cols = slice(b * SEG, (b + 1) * SEG)
             nc.sync.dma_start(out=out[h * P : (h + 1) * P, cols], in_=window[b][h][:, cols])
 
-        nc.vector.memset(pool_scales[:].bitcast(I32), 0)
         nc.sync.dma_start(offsets[:], offs)
         for quad in range(4):
-            nc.scalar.dma_start(
+            nc.sync.dma_start(
                 out=landed_scales[32 * quad : 32 * quad + 4, :].bitcast(I32),
                 in_=scales_hbm[4 * quad : 4 * quad + 4, :],
             )
+        load_do(0)
         load_words(0)
-        load_do(0, 0)
-        load_do(0, 1)
-        load_p(0, 0)
         nc.sync.dma_start(out=delta_sb[:], in_=delta.rearrange("b (s r) o -> s b (r o)", r=PACK))
-        load_p(0, 1)
+        load_p(0)
         load_q(0)
         load_words(1)
-        load_do(1, 0)
-        load_do(1, 1)
-        load_p(1, 0)
-        load_p(1, 1)
+        load_do(1)
         load_q(1)
+        load_p(1)
+
+        nc.vector.memset(pool_scales[:].bitcast(I32), 0)
         clear_window(0, 0)
         clear_window(0, 1)
-        clear_window(1, 0)
         for quad in range(4):
             rows = slice(32 * quad, 32 * quad + 4)
             nc.vector.tensor_copy(pool_scales[rows, :].bitcast(I32), landed_scales[rows, :].bitcast(I32))
 
-        steps = [(r, h) for r in range(PACK) for h in range(HALVES)]
-        gather_words(0)
         gather_scales(0)
+        gather_words(0)
         cast_do(0, 0)
         cast_do(0, 1)
         quantize_do(0)
         product_dp(0)
         gather_scales(1)
-        clear_window(1, 1, "do_raw01")
-        interleave(q_bf[0], q_raw[0])
-        form_ds(0, steps)
+        interleave(q_bf[0][:], q_raw[0][:])
+        form_ds(0)
         interleave_ds(0, 0)
         quantize_q(0)
         interleave_ds(0, 1, nc.vector.tensor_copy)
@@ -223,16 +214,17 @@ def tile_attend_bwd_seg_kernel(tc, doT, v_words, v_scales, p, delta, qm, offs, o
         quantize_ds(0, 1)
         product_dk(0)
         gather_words(1, "ds_bf00")
-        piece = copy_out(0, 0, 0, 320)
-        scatter(*piece)
+        clear_window(1, 0, nc.gpsimd, "ds_bf01")
+        clear_window(1, 1, nc.gpsimd, "ds_codes0")
+        scatter(*copy_out(0, 0, 0, 384))
         cast_do(1, 0)
         cast_do(1, 1)
         quantize_do(1)
         product_dp(1)
-        scatter(*copy_out(0, 0, 320, N, "do_raw11"))
+        scatter(*copy_out(0, 0, 384, N, "do_raw1"))
         store(0, 0)
-        interleave(q_bf[1], q_raw[1])
-        form_ds(1, steps)
+        interleave(q_bf[1][:], q_raw[1][:])
+        form_ds(1)
         piece = copy_out(0, 1, 0, 224, "p_sb10")
         interleave_ds(1, 0)
         interleave_ds(1, 1)
@@ -241,7 +233,7 @@ def tile_attend_bwd_seg_kernel(tc, doT, v_words, v_scales, p, delta, qm, offs, o
         quantize_ds(1, 0)
         quantize_ds(1, 1)
         product_dk(1)
-        scatter(*copy_out(0, 1, 224, N, "ds_rows11"))
+        scatter(*copy_out(0, 1, 224, N, "ds_rows1"))
         store(0, 1)
         for h in range(D // P):
             scatter(*copy_out(1, h, 0, N))

@@ -15,6 +15,7 @@ E4 = mybir.dt.float8_e4m3fn_x4
 E5 = mybir.dt.float8_e5m2_x4
 SUB = mybir.AluOpType.subtract
 MULT = mybir.AluOpType.mult
+IDENTITY = mybir.ActivationFunctionType.Identity
 
 P = 128
 PACK = 4
@@ -35,10 +36,11 @@ def tile_attend_bwd_seg_kernel(tc, doT, v_words, v_scales, p, delta, qm, offs, o
         offsets = sb.tile([P, B * N // LIST_ROWS], U16, name="offsets")
         pool_words = new("pool_words", [P, T], U32)
         pool_scales = new("pool_scales", [P, T], U8)
-        landed_scales = new("landed_scales", [P, T], U8)
         delta_sb = new("delta_sb", [P, B, PACK], F32)
-        do_raw = [new(f"do_raw{b}", [P, PACK, NQ], F32) for b in range(B)]
-        p_sb = [[new(f"p_sb{b}{h}", [P, PACK // HALVES, N], F32) for h in range(HALVES)] for b in range(B)]
+        do_raw = [[new(f"do_raw{b}{h}", [P, PACK, NQ // HALVES], F32) for h in range(HALVES)] for b in range(B)]
+        minus_delta = new("minus_delta", [P, B], F32)
+        shifted = [new(f"shifted{b}", [P, N], F32) for b in range(B)]
+        p_sb = [[new(f"p_sb{b}{r}", [P, N], F32) for r in range(PACK)] for b in range(B)]
         q_raw = [new(f"q_raw{b}", [P, PACK, D], F32) for b in range(B)]
         window = [{}, {}]
         v_codes = {}
@@ -65,29 +67,32 @@ def tile_attend_bwd_seg_kernel(tc, doT, v_words, v_scales, p, delta, qm, offs, o
         def half(h, width):
             return slice(h * width // HALVES, (h + 1) * width // HALVES)
 
-        def clear_window(b, h, engine=nc.vector, tag=None):
-            window[b][h] = new(f"window{b}{h}", [P, (b + 1) * SEG], F32, tag)
-            engine.memset(window[b][h][:, b * SEG : (b + 1) * SEG].bitcast(I32), 0)
+        def clear_window(b, h):
+            window[b][h] = new(f"window{b}{h}", [P, (b + 1) * SEG], F32)
+            nc.vector.memset(window[b][h][:, b * SEG : (b + 1) * SEG].bitcast(I32), 0)
 
         def load_words(b):
             cols = slice(b * SEG, (b + 1) * SEG)
             nc.sync.dma_start(out=pool_words[:, cols].bitcast(I32), in_=words_hbm[:, cols])
 
         def load_do(b):
-            nc.sync.dma_start(out=do_raw[b][:], in_=doT[b].rearrange("(g j) q -> g j q", j=PACK))
+            rows = doT[b].rearrange("(g j) (h q) -> h g j q", j=PACK, h=HALVES)
+            for h in range(HALVES):
+                nc.sync.dma_start(out=do_raw[b][h][:], in_=rows[h])
 
         def load_q(b):
             nc.sync.dma_start(out=q_raw[b][:], in_=qm[b].rearrange("(s r) d -> s r d", r=PACK))
 
-        def load_p(b):
+        def load_p(b, places):
             rows = p[b].rearrange("(s r) i -> s r i", r=PACK)
-            for h in range(HALVES):
-                nc.sync.dma_start(out=p_sb[b][h][:], in_=rows[:, half(h, PACK), :])
+            for r in places:
+                nc.sync.dma_start(out=p_sb[b][r][:], in_=rows[:, r, :])
 
-        def cast_do(b, h):
+        def cast_do(b, h, pair):
+            width = P // HALVES
             nc.scalar.copy(
-                out=do_bf[b][:, half(h, PACK), :, :].rearrange("g r s j -> g s j r"),
-                in_=do_raw[b][:].rearrange("g j (s r) -> g s j r", r=PACK)[:, :, :, half(h, PACK)],
+                out=do_bf[b][:, half(pair, PACK), h * width : (h + 1) * width, :].rearrange("g r s j -> g s j r"),
+                in_=do_raw[b][h][:].rearrange("g j (s r) -> g s j r", r=PACK)[:, :, :, half(pair, PACK)],
             )
 
         def interleave(dst, src, copy=nc.scalar.copy):
@@ -136,13 +141,15 @@ def tile_attend_bwd_seg_kernel(tc, doT, v_words, v_scales, p, delta, qm, offs, o
                 )
 
         def form_ds(b):
-            steps = [(r, slice(0, N)) for r in range(PACK - 1)] + [(PACK - 1, half(h, N)) for h in range(HALVES)]
+            nc.scalar.activation(out=shifted[b][:], in_=dp_ps[0][:], func=IDENTITY, bias=minus_delta[:, b : b + 1])
+            nc.gpsimd.tensor_tensor(out=ds_rows[b][:, 0, :], in0=shifted[b][:], in1=p_sb[b][0][:], op=MULT)
+            steps = [(r, slice(0, N)) for r in range(1, PACK - 1)] + [(PACK - 1, half(h, N)) for h in range(HALVES)]
             for r, cols in steps:
                 nc.vector.scalar_tensor_tensor(
                     out=ds_rows[b][:, r, cols],
                     in0=dp_ps[r][:, cols],
                     scalar=delta_sb[:, b, r : r + 1],
-                    in1=p_sb[b][r // HALVES][:, r % HALVES, cols],
+                    in1=p_sb[b][r][:, cols],
                     op0=SUB,
                     op1=MULT,
                 )
@@ -175,38 +182,38 @@ def tile_attend_bwd_seg_kernel(tc, doT, v_words, v_scales, p, delta, qm, offs, o
             cols = slice(b * SEG, (b + 1) * SEG)
             nc.sync.dma_start(out=out[h * P : (h + 1) * P, cols], in_=window[b][h][:, cols])
 
+        nc.vector.memset(pool_scales[:].bitcast(I32), 0)
         nc.sync.dma_start(offsets[:], offs)
         for quad in range(4):
             nc.sync.dma_start(
-                out=landed_scales[32 * quad : 32 * quad + 4, :].bitcast(I32),
+                out=pool_scales[32 * quad : 32 * quad + 4, :].bitcast(I32),
                 in_=scales_hbm[4 * quad : 4 * quad + 4, :],
             )
-        load_do(0)
-        load_words(0)
         nc.sync.dma_start(out=delta_sb[:], in_=delta.rearrange("b (s r) o -> s b (r o)", r=PACK))
-        load_p(0)
+        load_words(0)
+        load_do(0)
+        load_p(0, range(PACK - 1))
         load_q(0)
+        load_p(0, [PACK - 1])
         load_words(1)
         load_do(1)
         load_q(1)
-        load_p(1)
+        load_p(1, range(PACK))
+        for b in range(B):
+            for h in range(D // P):
+                clear_window(b, h)
 
-        nc.vector.memset(pool_scales[:].bitcast(I32), 0)
-        clear_window(0, 0)
-        clear_window(0, 1)
-        for quad in range(4):
-            rows = slice(32 * quad, 32 * quad + 4)
-            nc.vector.tensor_copy(pool_scales[rows, :].bitcast(I32), landed_scales[rows, :].bitcast(I32))
-
-        gather_scales(0)
         gather_words(0)
-        cast_do(0, 0)
-        cast_do(0, 1)
+        gather_scales(0)
+        for h in range(HALVES):
+            for pair in range(HALVES):
+                cast_do(0, h, pair)
+        nc.scalar.mul(minus_delta[:], delta_sb[:, :, 0], -1.0)
         quantize_do(0)
         product_dp(0)
         gather_scales(1)
-        interleave(q_bf[0][:], q_raw[0][:])
         form_ds(0)
+        interleave(q_bf[0][:], q_raw[0][:])
         interleave_ds(0, 0)
         quantize_q(0)
         interleave_ds(0, 1, nc.vector.tensor_copy)
@@ -214,22 +221,23 @@ def tile_attend_bwd_seg_kernel(tc, doT, v_words, v_scales, p, delta, qm, offs, o
         quantize_ds(0, 1)
         product_dk(0)
         gather_words(1, "ds_bf00")
-        clear_window(1, 0, nc.gpsimd, "ds_bf01")
-        clear_window(1, 1, nc.gpsimd, "ds_codes0")
-        scatter(*copy_out(0, 0, 0, 384))
-        cast_do(1, 0)
-        cast_do(1, 1)
+        cast_do(1, 0, 0)
+        cast_do(1, 0, 1)
+        scatter(*copy_out(0, 0, 0, 256, "do_raw10"))
+        cast_do(1, 1, 0)
+        cast_do(1, 1, 1)
         quantize_do(1)
         product_dp(1)
-        scatter(*copy_out(0, 0, 384, N, "do_raw1"))
-        store(0, 0)
-        interleave(q_bf[1][:], q_raw[1][:])
+        scatter(*copy_out(0, 0, 256, 384, "do_raw11"))
         form_ds(1)
-        piece = copy_out(0, 1, 0, 224, "p_sb10")
+        interleave(q_bf[1][:], q_raw[1][:])
+        pieces = [copy_out(0, 0, 384, N, "p_sb11"), copy_out(0, 1, 0, 224, "p_sb12")]
         interleave_ds(1, 0)
         interleave_ds(1, 1)
         quantize_q(1)
-        scatter(*piece)
+        for piece in pieces:
+            scatter(*piece)
+        store(0, 0)
         quantize_ds(1, 0)
         quantize_ds(1, 1)
         product_dk(1)

@@ -67,12 +67,12 @@ def tile_attend_bwd_seg_kernel(tc, doT, v_words, v_scales, p, delta, qm, offs, o
         def half(h, width):
             return slice(h * width // HALVES, (h + 1) * width // HALVES)
 
-        def clear_window(b, h):
-            window[b][h] = new(f"window{b}{h}", [P, (b + 1) * SEG], F32)
+        def clear_window(b, h, tag=None):
+            window[b][h] = new(f"window{b}{h}", [P, (b + 1) * SEG], F32, tag)
             nc.vector.memset(window[b][h][:, b * SEG : (b + 1) * SEG].bitcast(I32), 0)
 
-        def load_words(b):
-            cols = slice(b * SEG, (b + 1) * SEG)
+        def load_words(b, lo, hi):
+            cols = slice(b * SEG + lo, b * SEG + hi)
             nc.sync.dma_start(out=pool_words[:, cols].bitcast(I32), in_=words_hbm[:, cols])
 
         def load_do(b):
@@ -183,6 +183,8 @@ def tile_attend_bwd_seg_kernel(tc, doT, v_words, v_scales, p, delta, qm, offs, o
             nc.sync.dma_start(out=out[h * P : (h + 1) * P, cols], in_=window[b][h][:, cols])
 
         nc.vector.memset(pool_scales[:].bitcast(I32), 0)
+        load_words(0, 0, SEG // 2)
+        load_words(0, SEG // 2, SEG)
         nc.sync.dma_start(offsets[:], offs)
         for quad in range(4):
             nc.sync.dma_start(
@@ -190,18 +192,17 @@ def tile_attend_bwd_seg_kernel(tc, doT, v_words, v_scales, p, delta, qm, offs, o
                 in_=scales_hbm[4 * quad : 4 * quad + 4, :],
             )
         nc.sync.dma_start(out=delta_sb[:], in_=delta.rearrange("b (s r) o -> s b (r o)", r=PACK))
-        load_words(0)
         load_do(0)
         load_p(0, range(PACK - 1))
         load_q(0)
         load_p(0, [PACK - 1])
-        load_words(1)
+        load_words(1, 0, SEG)
         load_do(1)
         load_q(1)
         load_p(1, range(PACK))
-        for b in range(B):
-            for h in range(D // P):
-                clear_window(b, h)
+        clear_window(0, 0)
+        clear_window(0, 1)
+        clear_window(1, 0)
 
         gather_words(0)
         gather_scales(0)
@@ -212,6 +213,7 @@ def tile_attend_bwd_seg_kernel(tc, doT, v_words, v_scales, p, delta, qm, offs, o
         quantize_do(0)
         product_dp(0)
         gather_scales(1)
+        clear_window(1, 1, "do_raw01")
         form_ds(0)
         interleave(q_bf[0][:], q_raw[0][:])
         interleave_ds(0, 0)

from contextlib import ExitStack

import concourse.mybir as mybir

B, N, T, D, DV, NQ = 2, 512, 2048, 256, 512, 512
FLOPS = 2 * B * NQ * N * (DV + D)

F32 = mybir.dt.float32
BF16 = mybir.dt.bfloat16
I32 = mybir.dt.int32
U32 = mybir.dt.uint32
U16 = mybir.dt.uint16
U8 = mybir.dt.uint8
E4 = mybir.dt.float8_e4m3fn_x4
E5 = mybir.dt.float8_e5m2_x4
SUB = mybir.AluOpType.subtract
MULT = mybir.AluOpType.mult
IDENTITY = mybir.ActivationFunctionType.Identity

P = 128
PACK = 4
SEG = T // B
HALVES = 2
LIST_ROWS = 16


def tile_attend_bwd_seg_kernel(tc, doT, v_words, v_scales, p, delta, qm, offs, out):
    nc = tc.nc
    with ExitStack() as ctx:
        sb = ctx.enter_context(tc.tile_pool(name="sb", bufs=1))
        ps = ctx.enter_context(tc.psum_pool(name="ps", bufs=1))

        def new(name, shape, dtype, tag=None):
            return sb.tile(shape, dtype, name=name, tag=tag or name, align_bytes=64)

        offsets = sb.tile([P, B * N // LIST_ROWS], U16, name="offsets")
        pool_words = new("pool_words", [P, T], U32)
        pool_scales = new("pool_scales", [P, T], U8)
        delta_sb = new("delta_sb", [P, B, PACK], F32)
        do_raw = [[new(f"do_raw{b}{h}", [P, PACK, NQ // HALVES], F32) for h in range(HALVES)] for b in range(B)]
        minus_delta = new("minus_delta", [P, B], F32)
        shifted = [new(f"shifted{b}", [P, N], F32) for b in range(B)]
        p_sb = [[new(f"p_sb{b}{r}", [P, N], F32) for r in range(PACK)] for b in range(B)]
        q_raw = [new(f"q_raw{b}", [P, PACK, D], F32) for b in range(B)]
        window = [{}, {}]
        v_codes = {}
        v_plane = [new(f"v_plane{b}", [P, N], U8) for b in range(B)]
        do_bf = [new(f"do_bf{b}", [P, PACK, P, PACK], BF16) for b in range(B)]
        do_codes = [new(f"do_codes{b}", [P, NQ], U32) for b in range(B)]
        do_plane = [new(f"do_plane{b}", [P, NQ], U8) for b in range(B)]
        q_bf = [new(f"q_bf{b}", [P, D, PACK], BF16) for b in range(B)]
        q_codes = [new(f"q_codes{b}", [P, D], U32) for b in range(B)]
        q_plane = [new(f"q_plane{b}", [P, D], U8) for b in range(B)]
        ds_rows = [new(f"ds_rows{b}", [P, PACK, N], BF16) for b in range(B)]
        ds_bf = [[new(f"ds_bf{b}{h}", [P, N // HALVES, PACK], BF16) for h in range(HALVES)] for b in range(B)]
        ds_codes = [new(f"ds_codes{b}", [P, N], U32) for b in range(B)]
        ds_plane = [new(f"ds_plane{b}", [P, N], U8) for b in range(B)]
        dp_ps = [ps.tile([P, N], F32, name=f"dp_ps{r}") for r in range(PACK)]
        dk_ps = [[ps.tile([P, N], F32, name=f"dk_ps{b}{h}") for h in range(D // P)] for b in range(B)]

        words_hbm = v_words[0].rearrange("g t r -> g (t r)").bitcast(I32)
        scales_hbm = v_scales[0].bitcast(I32)

        def slots(b, lo=0, hi=N):
            return offsets[:, (b * N + lo) // LIST_ROWS : (b * N + hi) // LIST_ROWS]

        def half(h, width):
            return slice(h * width // HALVES, (h + 1) * width // HALVES)

        def clear_window(b, h, tag=None):
            window[b][h] = new(f"window{b}{h}", [P, (b + 1) * SEG], F32, tag)
            nc.vector.memset(window[b][h][:, b * SEG : (b + 1) * SEG].bitcast(I32), 0)

        def load_words(b, lo, hi):
            cols = slice(b * SEG + lo, b * SEG + hi)
            nc.sync.dma_start(out=pool_words[:, cols].bitcast(I32), in_=words_hbm[:, cols])

        def load_do(b):
            rows = doT[b].rearrange("(g j) (h q) -> h g j q", j=PACK, h=HALVES)
            for h in range(HALVES):
                nc.sync.dma_start(out=do_raw[b][h][:], in_=rows[h])

        def load_q(b):
            nc.sync.dma_start(out=q_raw[b][:], in_=qm[b].rearrange("(s r) d -> s r d", r=PACK))

        def load_p(b, places):
            rows = p[b].rearrange("(s r) i -> s r i", r=PACK)
            for r in places:
                nc.sync.dma_start(out=p_sb[b][r][:], in_=rows[:, r, :])

        def cast_do(b, h, pair):
            width = P // HALVES
            nc.scalar.copy(
                out=do_bf[b][:, half(pair, PACK), h * width : (h + 1) * width, :].rearrange("g r s j -> g s j r"),
                in_=do_raw[b][h][:].rearrange("g j (s r) -> g s j r", r=PACK)[:, :, :, half(pair, PACK)],
            )

        def interleave(dst, src, copy=nc.scalar.copy):
            copy(out=dst, in_=src.rearrange("s r x -> s x r"))

        def gather_words(b, tag=None):
            v_codes[b] = new(f"v_codes{b}", [P, N], U32, tag)
            nc.vector.tensor_copy(v_codes[b][:], pool_words[:, 0 : (b + 1) * SEG].indirect(slots(b)))

        def gather_scales(b):
            nc.vector.tensor_copy(v_plane[b][:], pool_scales[:, 0 : (b + 1) * SEG].indirect(slots(b)))

        def quantize_do(b):
            for h in range(HALVES):
                nc.vector.quantize_mx(
                    out=do_codes[b][:, half(h, NQ)].bitcast(E5),
                    scales=do_plane[b][:, half(h, NQ)],
                    in_=do_bf[b][:, half(h, PACK), :, :].rearrange("g r s j -> g (r s j)"),
                )

        def quantize_q(b):
            nc.vector.quantize_mx(
                out=q_codes[b][:].bitcast(E4),
                scales=q_plane[b][:],
                in_=q_bf[b][:].rearrange("s d r -> s (d r)"),
            )

        def quantize_ds(b, h):
            nc.vector.quantize_mx(
                out=ds_codes[b][:, half(h, N)].bitcast(E5),
                scales=ds_plane[b][:, half(h, N)],
                in_=ds_bf[b][h][:].rearrange("s i r -> s (i r)"),
            )

        def product_dp(b):
            for r in range(PACK):
                cols = slice(r * P, (r + 1) * P)
                nc.tensor.matmul_mx(
                    out=dp_ps[r][:],
                    lhsT=do_codes[b][:, cols].bitcast(E5),
                    lhsT_scale=do_plane[b][:, cols],
                    rhs=v_codes[b][:].bitcast(E4),
                    rhs_scale=v_plane[b][:],
                    start=True,
                    stop=True,
                )

        def form_ds(b):
            nc.scalar.activation(out=shifted[b][:], in_=dp_ps[0][:], func=IDENTITY, bias=minus_delta[:, b : b + 1])
            nc.gpsimd.tensor_tensor(out=ds_rows[b][:, 0, :], in0=shifted[b][:], in1=p_sb[b][0][:], op=MULT)
            steps = [(r, slice(0, N)) for r in range(1, PACK - 1)] + [(PACK - 1, half(h, N)) for h in range(HALVES)]
            for r, cols in steps:
                nc.vector.scalar_tensor_tensor(
                    out=ds_rows[b][:, r, cols],
                    in0=dp_ps[r][:, cols],
                    scalar=delta_sb[:, b, r : r + 1],
                    in1=p_sb[b][r][:, cols],
                    op0=SUB,
                    op1=MULT,
                )

        def interleave_ds(b, h, copy=nc.scalar.copy):
            interleave(ds_bf[b][h][:], ds_rows[b][:, :, half(h, N)], copy)

        def product_dk(b):
            for h in range(D // P):
                cols = slice(h * P, (h + 1) * P)
                nc.tensor.matmul_mx(
                    out=dk_ps[b][h][:],
                    lhsT=q_codes[b][:, cols].bitcast(E4),
                    lhsT_scale=q_plane[b][:, cols],
                    rhs=ds_codes[b][:].bitcast(E5),
                    rhs_scale=ds_plane[b][:],
                    start=True,
                    stop=True,
                )

        def copy_out(b, h, lo, hi, tag=None):
            staged = new(f"dk_sb{b}{h}_{lo}", [P, hi - lo], F32, tag)
            nc.scalar.copy(out=staged[:], in_=dk_ps[b][h][:, lo:hi])
            return b, h, lo, hi, staged

        def scatter(b, h, lo, hi, staged):
            nc.vector.tensor_copy(window[b][h][:].indirect(slots(b, lo, hi)), staged[:])

        def store(b, h):
            cols = slice(b * SEG, (b + 1) * SEG)
            nc.sync.dma_start(out=out[h * P : (h + 1) * P, cols], in_=window[b][h][:, cols])

        nc.vector.memset(pool_scales[:].bitcast(I32), 0)
        load_words(0, 0, SEG // 2)
        load_words(0, SEG // 2, SEG)
        nc.sync.dma_start(offsets[:], offs)
        for quad in range(4):
            nc.sync.dma_start(
                out=pool_scales[32 * quad : 32 * quad + 4, :].bitcast(I32),
                in_=scales_hbm[4 * quad : 4 * quad + 4, :],
            )
        nc.sync.dma_start(out=delta_sb[:], in_=delta.rearrange("b (s r) o -> s b (r o)", r=PACK))
        load_do(0)
        load_p(0, range(PACK - 1))
        load_q(0)
        load_p(0, [PACK - 1])
        load_words(1, 0, SEG)
        load_do(1)
        load_q(1)
        load_p(1, range(PACK))
        clear_window(0, 0)
        clear_window(0, 1)
        clear_window(1, 0)

        gather_words(0)
        gather_scales(0)
        for h in range(HALVES):
            for pair in range(HALVES):
                cast_do(0, h, pair)
        nc.scalar.mul(minus_delta[:], delta_sb[:, :, 0], -1.0)
        quantize_do(0)
        product_dp(0)
        gather_scales(1)
        clear_window(1, 1, "do_raw01")
        form_ds(0)
        interleave(q_bf[0][:], q_raw[0][:])
        interleave_ds(0, 0)
        quantize_q(0)
        interleave_ds(0, 1, nc.vector.tensor_copy)
        quantize_ds(0, 0)
        quantize_ds(0, 1)
        product_dk(0)
        gather_words(1, "ds_bf00")
        cast_do(1, 0, 0)
        cast_do(1, 0, 1)
        scatter(*copy_out(0, 0, 0, 256, "do_raw10"))
        cast_do(1, 1, 0)
        cast_do(1, 1, 1)
        quantize_do(1)
        product_dp(1)
        scatter(*copy_out(0, 0, 256, 384, "do_raw11"))
        form_ds(1)
        interleave(q_bf[1][:], q_raw[1][:])
        pieces = [copy_out(0, 0, 384, N, "p_sb11"), copy_out(0, 1, 0, 224, "p_sb12")]
        interleave_ds(1, 0)
        interleave_ds(1, 1)
        quantize_q(1)
        for piece in pieces:
            scatter(*piece)
        store(0, 0)
        quantize_ds(1, 0)
        quantize_ds(1, 1)
        product_dk(1)
        scatter(*copy_out(0, 1, 224, N, "ds_rows1"))
        store(0, 1)
        for h in range(D // P):
            scatter(*copy_out(1, h, 0, N))
            store(1, h)
